import numpy as np
import ml_dtypes


def mxq(x, axis, fmt="e4m3"):
    dtype, down = {"e4m3": (ml_dtypes.float8_e4m3fn, 7), "e5m2": (ml_dtypes.float8_e5m2, 14)}[fmt]
    v = np.moveaxis(np.asarray(x, np.float32).astype(ml_dtypes.bfloat16).astype(np.float64), axis, -1)
    blocks = v.reshape(v.shape[:-1] + (-1, 32))
    amax = np.abs(blocks).max(-1, keepdims=True)
    byte = np.maximum(np.where(amax > 0, np.frexp(amax)[1] - 1 + 127, 0) - down, 1)
    scale = np.exp2(byte - 127.0)
    codes = (blocks / scale).astype(np.float32).astype(dtype).astype(np.float64)
    return np.moveaxis((codes * scale).reshape(v.shape), -1, axis)


WIDE = False


def mx_kscale(k):
    if not WIDE:
        return np.ones(k)
    levels = np.array([10, -10, 5, -5, 0])
    if k % 512:
        return np.exp2(np.random.permutation(np.resize(levels, k // 32))).repeat(32)
    a = np.empty((k // 512, 16))
    for p in range(k // 512):
        a[p, :8] = np.random.permutation(np.resize(levels, 8))
        for g in range(8):
            far = levels[np.abs(levels - a[p, g]) >= 10]
            a[p, g + 8] = far[np.random.randint(len(far))]
    return np.exp2(a.ravel()).repeat(32)


def f64(x):
    return np.asarray(x).astype(np.float64)


def striped(idx):
    return np.tile(idx.reshape(-1, 16).T, (8, 1)).astype(np.uint16)


def unstriped(offs):
    return offs[:16].T.reshape(-1).astype(np.int64)


def striped8(idx):
    return np.concatenate([x.reshape(-1, 16).T for x in idx]).astype(np.uint16)


def runs(offs, k):
    lists = np.stack([offs[16 * r : 16 * r + 16].T.reshape(-1) for r in range(8)]).astype(np.int64)
    return lists[np.arange(k) % 512 // 64]


def pack_weight(w):
    k, n = w.shape
    w = f64(np.asarray(w, np.float32).astype(ml_dtypes.bfloat16)).reshape(k // 32, 32, n)
    amax = np.abs(w).max(1)
    byte = np.clip(np.where(amax > 0, np.frexp(amax)[1] - 1 + 127 - 7, 1), 1, 254)
    scaled = (w * np.exp2(127.0 - byte)[:, None, :]).reshape(k, n).astype(np.float32)
    words = np.ascontiguousarray(scaled.reshape(k // 512, 128, 4, n).transpose(0, 1, 3, 2)).astype(ml_dtypes.float8_e4m3fn).view(np.uint8)
    return words, np.ascontiguousarray(byte.astype(np.uint8).reshape(k // 512, 16, n))


def unpack_weight(words, scales):
    g, p, n, _ = words.shape
    vals = np.ascontiguousarray(words).view(ml_dtypes.float8_e4m3fn).astype(np.float64) * np.repeat(np.exp2(scales.astype(np.float64) - 127.0), 8, axis=1)[..., None]
    return vals.transpose(0, 1, 3, 2).reshape(g * 512, n)


def sigmoid(v):
    return 1.0 / (1.0 + np.exp(-np.maximum(v, -700.0)))


K, T, S, H, C = 512, 2048, 512, 512, 512


def setup_inputs():
    n = np.random.standard_normal
    s = mx_kscale(K)[:, None]
    packed_xT = pack_weight(n((K, T)) * s)
    return {
        "x_words": packed_xT[0],
        "x_scales": packed_xT[1],
        "w1": (n((K, H)) / np.sqrt(K) / s).astype(np.float32),
        "gs": (np.random.uniform(0.5, 1.5, (K, 1)) / s).astype(np.float32),
        "offs": striped(np.random.permutation(T)[:S]),
        "n1": striped8(np.stack([np.random.permutation(S) for _ in range(8)])),
        "n2": striped8(np.stack([np.random.permutation(S) for _ in range(8)])),
        "ca": striped(np.random.permutation(T)[:C]),
        "cb": striped(np.random.permutation(T)[:C]),
        "n3": striped8(np.stack([np.random.permutation(S) for _ in range(8)])),
        "n4": striped8(np.stack([np.random.permutation(S) for _ in range(8)])),
        "n5": striped8(np.stack([np.random.permutation(S) for _ in range(8)])),
    }


def reference(x_words, x_scales, w1, gs, offs, n1, n2, ca, cb, n3, n4, n5):
    x_ca = unpack_weight(x_words, x_scales)[:, unstriped(ca)]
    xq = unpack_weight(x_words, x_scales)[:, unstriped(offs)]
    y = mxq(f64(w1), 0, "e4m3").T @ xq
    st = y[np.arange(H)[:, None], runs(n1, H)] - y
    z = f64(gs) * (y * (sigmoid(st[np.arange(H)[:, None], runs(n2, H)])))
    zq = mxq(z, 0, "e4m3")
    a = 0.0625 * (x_ca.T @ zq)
    x_cb = unpack_weight(x_words, x_scales)[:, unstriped(cb)]
    b = 0.0625 * (x_cb.T @ zq)
    return np.maximum(np.minimum(a - (0.5 * (a[np.arange(C)[:, None], runs(n3, C)])), b[np.arange(C)[:, None], runs(n4, C)]), b[np.arange(C)[:, None], runs(n5, C)])

@@ -1,0 +1,198 @@
+from contextlib import ExitStack
+
+import concourse.mybir as mybir
+from concourse.masks import make_identity
+
+F32 = mybir.dt.float32
+BF16 = mybir.dt.bfloat16
+I32 = mybir.dt.int32
+U32 = mybir.dt.uint32
+U16 = mybir.dt.uint16
+U8 = mybir.dt.uint8
+FP8X4 = mybir.dt.float8_e4m3fn_x4
+ALU = mybir.AluOpType
+ACT = mybir.ActivationFunctionType
+
+P = 128
+T = 2048
+S = 512
+PACK = 4
+WINDOW = 1024
+W_CHUNKS = 2
+FLOPS = 3 * 2 * 512 * 512 * 512
+
+
+def tile_picked_ccmpclampbhopd_none_p_kernel(tc, x_words, x_scales, w1, gs, offs, n1, n2, ca, cb, n3, n4, n5, out):
+    nc = tc.nc
+    with ExitStack() as ctx:
+        keep = ctx.enter_context(tc.tile_pool(name="keep", bufs=1))
+        psum = ctx.enter_context(tc.psum_pool(name="psum", bufs=1))
+
+        def load_list(src, name):
+            tile = keep.tile([P, S // 16], U16, name=name)
+            nc.sync.dma_start(tile[:], src)
+            return tile
+
+        scales = keep.tile([P, T], U8, name="scales")
+        nc.gpsimd.memset(scales[:].bitcast(I32), 0)
+        warm = keep.tile([P, 8], F32, name="warm")
+        nc.vector.memset(warm[:, 0:1], 0.0)
+
+        offs_sb = load_list(offs, "offs_sb")
+        ca_sb = load_list(ca, "ca_sb")
+        cb_sb = load_list(cb, "cb_sb")
+        words = keep.tile([P, T], U32, name="words")
+        nc.sync.dma_start(words[:].bitcast(I32), x_words[0].rearrange("p n t -> p (n t)").bitcast(I32))
+        for q in range(4):
+            nc.scalar.dma_start(scales[32 * q : 32 * q + 4, :].bitcast(I32), x_scales[0, 4 * q : 4 * q + 4, :].bitcast(I32))
+        nc.scalar.activation(warm[:, 1:2], warm[:, 0:1], ACT.Sigmoid)
+        cw = S // W_CHUNKS
+        w_rows = w1.rearrange("(p j) c -> p j c", j=PACK)
+        w_raw = []
+        for h in range(W_CHUNKS):
+            tile = keep.tile([P, PACK, cw], F32, name="w_raw%d" % h)
+            nc.sync.dma_start(tile[:], w_rows[:, :, h * cw : (h + 1) * cw])
+            w_raw.append(tile)
+        n1_sb = load_list(n1, "n1_sb")
+        n2_sb = load_list(n2, "n2_sb")
+        gs_sb = keep.tile([P, PACK], F32, name="gs_sb")
+        nc.sync.dma_start(gs_sb[:], gs.rearrange("(p t) o -> p (t o)", t=PACK))
+        n3_sb = load_list(n3, "n3_sb")
+        n4_sb = load_list(n4, "n4_sb")
+        n5_sb = load_list(n5, "n5_sb")
+
+        xq_s = keep.tile([P, S], U8, name="xq_s", align_bytes=64)
+        nc.vector.tensor_copy(xq_s[:], scales[:].indirect(offs_sb[:]))
+        dealt_s = []
+        for name, lst in (("a", ca_sb), ("b", cb_sb)):
+            plain = keep.tile([P, S], U8, name="plain_s" + name, align_bytes=64)
+            nc.vector.tensor_copy(plain[:], scales[:].indirect(lst[:]))
+            dealt = keep.tile([P, S], U8, name="dealt_s" + name, align_bytes=64)
+            nc.vector.tensor_copy(
+                dealt[:].bitcast(I32).rearrange("p (t g q) -> p t g q", t=4, g=8),
+                plain[:].bitcast(I32).rearrange("p (g t q) -> p t g q", t=4, g=8),
+            )
+            dealt_s.append(dealt)
+        xq_w = keep.tile([P, S], U32, name="xq_w", align_bytes=64)
+        nc.vector.tensor_copy(xq_w[:], words[:].indirect(offs_sb[:]))
+
+        w_bf = keep.tile([P, PACK, P, PACK], BF16, name="w_bf", tag="w_then_words", align_bytes=64)
+        mw = cw // PACK
+        for h in range(W_CHUNKS):
+            nc.scalar.copy(
+                w_bf[:, :, h * mw : (h + 1) * mw, :].rearrange("p t m j -> p m j t"),
+                w_raw[h][:].rearrange("p j (m t) -> p m j t", t=PACK),
+            )
+        w_w = keep.tile([P, S], U32, name="w_w", align_bytes=64)
+        w_s = keep.tile([P, S], U8, name="w_s", align_bytes=64)
+        nc.vector.quantize_mx(out=w_w[:].bitcast(FP8X4), scales=w_s[:], in_=w_bf[:].rearrange("p t m j -> p (t m j)"))
+
+        dealt_w = keep.tile([P, 2, S], U32, name="dealt_w", tag="w_then_words", align_bytes=64)
+        for k, lst in enumerate((ca_sb, cb_sb)):
+            nc.vector.tensor_copy(dealt_w[:, k, :].rearrange("p (t g q) -> p g t q", t=4, g=8), words[:].indirect(lst[:]))
+        ident = keep.tile([P, P], F32, name="ident")
+        make_identity(nc, ident[:])
+
+        banks = [psum.tile([P, S], F32, name="bank%d" % b) for b in range(8)]
+        win_a = [keep.tile([P, WINDOW], F32, name="win_a%d" % t) for t in range(PACK)]
+        win_b = [keep.tile([P, WINDOW], F32, name="win_b%d" % t) for t in range(PACK)]
+        plain_y = [keep.tile([P, S], F32, name="plain_y%d" % t) for t in range(PACK)]
+        sig = [keep.tile([P, S], F32, name="sig%d" % t) for t in range(PACK)]
+        z_bf = keep.tile([P, PACK, S], BF16, name="z_bf")
+
+        for t in range(PACK):
+            cols = slice(t * P, (t + 1) * P)
+            nc.tensor.matmul_mx(out=banks[t][:], lhsT=w_w[:, cols].bitcast(FP8X4), lhsT_scale=w_s[:, cols],
+                                rhs=xq_w[:].bitcast(FP8X4), rhs_scale=xq_s[:], start=True, stop=True)
+        for t in range(PACK):
+            nc.scalar.copy(win_a[t][:, :S], banks[t][:])
+            if t < 2:
+                nc.scalar.copy(plain_y[t][:], banks[t][:])
+            else:
+                nc.vector.tensor_copy(plain_y[t][:], win_a[t][:, :S])
+        for t in range(PACK):
+            nc.vector.tensor_tensor(win_b[t][:, :S], win_a[t][:].indirect(n1_sb[:]), plain_y[t][:], ALU.subtract)
+        for t in range(PACK):
+            nc.scalar.activation(sig[t][:], win_b[t][:].indirect(n2_sb[:]), ACT.Sigmoid)
+        for t in range(PACK):
+            nc.vector.scalar_tensor_tensor(z_bf[:, t, :], plain_y[t][:], gs_sb[:, t : t + 1], sig[t][:], ALU.mult, ALU.mult)
+
+        z_il = [keep.tile([P, S // 2, PACK], BF16, name="z_il%d" % h, align_bytes=64) for h in range(2)]
+        z_w = keep.tile([P, S], U32, name="z_w", align_bytes=64)
+        z_s = keep.tile([P, S], U8, name="z_s", align_bytes=64)
+        halves = (slice(0, S // 2), slice(S // 2, S))
+        for engine_copy, half, cols in zip((nc.vector.tensor_copy, nc.scalar.copy), z_il, halves):
+            engine_copy(half[:].rearrange("p (c i) t -> p c t i", i=4), z_bf[:, :, cols].rearrange("p t (c i) -> p c t i", i=4))
+        for half, cols in zip(z_il, halves):
+            nc.vector.quantize_mx(out=z_w[:, cols].bitcast(FP8X4), scales=z_s[:, cols], in_=half[:].rearrange("p c t -> p (c t)"))
+
+        def product(bank, k, t, cols):
+            rows = slice(t * P, (t + 1) * P)
+            nc.tensor.matmul_mx(out=bank[:, cols], lhsT=dealt_w[:, k, rows].bitcast(FP8X4), lhsT_scale=dealt_s[k][:, rows],
+                                rhs=z_w[:, cols].bitcast(FP8X4), rhs_scale=z_s[:, cols], start=True, stop=True)
+
+        out_rows = out.rearrange("(g t q) j -> t g q j", t=4, g=8)
+        whole = slice(0, S)
+        plain_a = [keep.tile([P, S], F32, name="plain_a%d" % t) for t in range(PACK)]
+        u = [keep.tile([P, S], F32, name="u%d" % t) for t in range(PACK)]
+        d4 = [keep.tile([P, S], F32, name="d4_%d" % t) for t in range(PACK)]
+        d5 = [keep.tile([P, S], F32, name="d5_%d" % t) for t in range(PACK)]
+        res = [keep.tile([P, S], F32, name="res%d" % t) for t in range(PACK)]
+        turned = [keep.tile([P, S], F32, name="turned%d" % t) for t in range(PACK - 1)]
+        ab_banks = ((4, 5), (0, 1), (2, 3), (4, 5))
+
+        def scores(t):
+            bank_a, bank_b = banks[ab_banks[t][0]], banks[ab_banks[t][1]]
+            if t == 0:
+                for bank, cols in zip((bank_a, banks[6]), halves):
+                    product(bank, 0, t, cols)
+                    nc.scalar.activation(win_a[t][:, cols], bank[:, cols], ACT.Copy, scale=-0.5 * 0.0625)
+                    nc.vector.tensor_scalar(plain_a[t][:, cols], win_a[t][:, cols], -2.0, None, ALU.mult)
+            else:
+                product(bank_a, 0, t, whole)
+                nc.scalar.activation(win_a[t][:, :S], bank_a[:], ACT.Copy, scale=-0.5 * 0.0625)
+                nc.scalar.activation(plain_a[t][:], bank_a[:], ACT.Copy, scale=0.0625)
+            product(bank_b, 1, t, whole)
+            nc.scalar.activation(win_b[t][:, :S], bank_b[:], ACT.Copy, scale=0.0625)
+
+        def first_gather(t):
+            nc.vector.tensor_tensor(u[t][:], win_a[t][:].indirect(n3_sb[:]), plain_a[t][:], ALU.add)
+
+        def b_gathers(t):
+            nc.vector.tensor_tensor(d4[t][:], win_b[t][:].indirect(n4_sb[:]), u[t][:], ALU.subtract)
+            nc.vector.tensor_tensor(d5[t][:], win_b[t][:].indirect(n5_sb[:]), u[t][:], ALU.subtract)
+
+        def clamp(t):
+            nc.vector.scalar_tensor_tensor(d4[t][:], d4[t][:], 0.0, d5[t][:], ALU.min, ALU.max)
+
+        def add_and_store(t):
+            for h, half in enumerate(halves):
+                blocks = [slice(c * P, (c + 1) * P) for c in (2 * h, 2 * h + 1)]
+                for cols in blocks:
+                    nc.tensor.matmul(banks[6 + h][:, cols], u[t][:, cols], ident[:], start=True, stop=False, is_transpose=True)
+                    nc.tensor.matmul(banks[6 + h][:, cols], d4[t][:, cols], ident[:], start=False, stop=True, is_transpose=True)
+                nc.scalar.copy(turned[t][:, half], banks[6 + h][:, half])
+            for h, half in enumerate(halves):
+                blocks = [slice(c * P, (c + 1) * P) for c in (2 * h, 2 * h + 1)]
+                for cols in blocks:
+                    nc.tensor.transpose(banks[h][:, cols], turned[t][:, cols], ident[:])
+                nc.scalar.copy(res[t][:, half], banks[h][:, half])
+                nc.sync.dma_start(out_rows[t][:, :, half], res[t][:, half])
+
+        scores(0)
+        scores(1)
+        first_gather(0)
+        for t in range(PACK - 1):
+            b_gathers(t)
+            if t + 2 < PACK:
+                scores(t + 2)
+            first_gather(t + 1)
+            clamp(t)
+            add_and_store(t)
+        t = PACK - 1
+        nc.vector.tensor_copy(d4[t][:], win_b[t][:].indirect(n4_sb[:]))
+        nc.vector.tensor_copy(d5[t][:], win_b[t][:].indirect(n5_sb[:]))
+        nc.vector.tensor_tensor(d4[t][:], d4[t][:], u[t][:], ALU.min)
+        for cols in halves:
+            nc.vector.tensor_tensor(res[t][:, cols], d4[t][:, cols], d5[t][:, cols], ALU.max)
+            nc.sync.dma_start(out_rows[t][:, :, cols], res[t][:, cols])

@@ -34,18 +34,16 @@ def tile_picked_ccmpclampbhopd_none_p_kernel(tc, x_words, x_scales, w1, gs, offs
             return tile
 
         scales = keep.tile([P, T], U8, name="scales")
-        nc.gpsimd.memset(scales[:].bitcast(I32), 0)
+        nc.vector.memset(scales[:].bitcast(I32), 0)
         warm = keep.tile([P, 8], F32, name="warm")
-        nc.vector.memset(warm[:, 0:1], 0.0)
+        nc.gpsimd.memset(warm[:, 0:1], 0.0)
+        nc.scalar.activation(warm[:, 1:2], warm[:, 0:1], ACT.Sigmoid)
 
         offs_sb = load_list(offs, "offs_sb")
         ca_sb = load_list(ca, "ca_sb")
         cb_sb = load_list(cb, "cb_sb")
-        words = keep.tile([P, T], U32, name="words")
-        nc.sync.dma_start(words[:].bitcast(I32), x_words[0].rearrange("p n t -> p (n t)").bitcast(I32))
         for q in range(4):
-            nc.scalar.dma_start(scales[32 * q : 32 * q + 4, :].bitcast(I32), x_scales[0, 4 * q : 4 * q + 4, :].bitcast(I32))
-        nc.scalar.activation(warm[:, 1:2], warm[:, 0:1], ACT.Sigmoid)
+            nc.sync.dma_start(scales[32 * q : 32 * q + 4, :].bitcast(I32), x_scales[0, 4 * q : 4 * q + 4, :].bitcast(I32))
         cw = S // W_CHUNKS
         w_rows = w1.rearrange("(p j) c -> p j c", j=PACK)
         w_raw = []
@@ -53,6 +51,8 @@ def tile_picked_ccmpclampbhopd_none_p_kernel(tc, x_words, x_scales, w1, gs, offs
             tile = keep.tile([P, PACK, cw], F32, name="w_raw%d" % h)
             nc.sync.dma_start(tile[:], w_rows[:, :, h * cw : (h + 1) * cw])
             w_raw.append(tile)
+        words = keep.tile([P, T], U32, name="words", align_bytes=64)
+        nc.sync.dma_start(words[:].bitcast(I32), x_words[0].rearrange("p n t -> p (n t)").bitcast(I32))
         n1_sb = load_list(n1, "n1_sb")
         n2_sb = load_list(n2, "n2_sb")
         gs_sb = keep.tile([P, PACK], F32, name="gs_sb")
@@ -61,35 +61,47 @@ def tile_picked_ccmpclampbhopd_none_p_kernel(tc, x_words, x_scales, w1, gs, offs
         n4_sb = load_list(n4, "n4_sb")
         n5_sb = load_list(n5, "n5_sb")
 
-        xq_s = keep.tile([P, S], U8, name="xq_s", align_bytes=64)
-        nc.vector.tensor_copy(xq_s[:], scales[:].indirect(offs_sb[:]))
-        dealt_s = []
-        for name, lst in (("a", ca_sb), ("b", cb_sb)):
-            plain = keep.tile([P, S], U8, name="plain_s" + name, align_bytes=64)
-            nc.vector.tensor_copy(plain[:], scales[:].indirect(lst[:]))
-            dealt = keep.tile([P, S], U8, name="dealt_s" + name, align_bytes=64)
+        def dealt_words(lst, name, tag):
+            dealt = keep.tile([P, S], U32, name=name, tag=tag, align_bytes=64)
+            nc.vector.tensor_copy(dealt[:].rearrange("p (t g q) -> p g t q", t=4, g=8), words[:].indirect(lst[:]))
+            return dealt
+
+        def gathered_bytes(lst, name):
+            picked = keep.tile([P, S], U8, name=name, align_bytes=64)
+            nc.vector.tensor_copy(picked[:], scales[:].indirect(lst[:]))
+            return picked
+
+        def dealt_bytes(picked, name):
+            dealt = keep.tile([P, S], U8, name=name, align_bytes=64)
             nc.vector.tensor_copy(
                 dealt[:].bitcast(I32).rearrange("p (t g q) -> p t g q", t=4, g=8),
-                plain[:].bitcast(I32).rearrange("p (g t q) -> p t g q", t=4, g=8),
+                picked[:].bitcast(I32).rearrange("p (g t q) -> p t g q", t=4, g=8),
             )
-            dealt_s.append(dealt)
-        xq_w = keep.tile([P, S], U32, name="xq_w", align_bytes=64)
-        nc.vector.tensor_copy(xq_w[:], words[:].indirect(offs_sb[:]))
+            return dealt
 
-        w_bf = keep.tile([P, PACK, P, PACK], BF16, name="w_bf", tag="w_then_words", align_bytes=64)
+        halves = (slice(0, S // 2), slice(S // 2, S))
+        whole = slice(0, S)
+        xq_s = gathered_bytes(offs_sb, "xq_s")
+        a_picked = gathered_bytes(ca_sb, "a_picked")
+        b_picked = gathered_bytes(cb_sb, "b_picked")
+        a_bytes = dealt_bytes(a_picked, "a_bytes")
+        b_bytes = dealt_bytes(b_picked, "b_bytes")
+
+        w_bf = keep.tile([P, PACK, P, PACK], BF16, name="w_bf", align_bytes=64)
         mw = cw // PACK
         for h in range(W_CHUNKS):
             nc.scalar.copy(
-                w_bf[:, :, h * mw : (h + 1) * mw, :].rearrange("p t m j -> p m j t"),
-                w_raw[h][:].rearrange("p j (m t) -> p m j t", t=PACK),
+                w_bf[:, :, h * mw : (h + 1) * mw, :].rearrange("p t m j -> p m t j"),
+                w_raw[h][:].rearrange("p j (m t) -> p m t j", t=PACK),
             )
         w_w = keep.tile([P, S], U32, name="w_w", align_bytes=64)
         w_s = keep.tile([P, S], U8, name="w_s", align_bytes=64)
         nc.vector.quantize_mx(out=w_w[:].bitcast(FP8X4), scales=w_s[:], in_=w_bf[:].rearrange("p t m j -> p (t m j)"))
 
-        dealt_w = keep.tile([P, 2, S], U32, name="dealt_w", tag="w_then_words", align_bytes=64)
-        for k, lst in enumerate((ca_sb, cb_sb)):
-            nc.vector.tensor_copy(dealt_w[:, k, :].rearrange("p (t g q) -> p g t q", t=4, g=8), words[:].indirect(lst[:]))
+        xq_w = keep.tile([P, S], U32, name="xq_w", align_bytes=64)
+        for h, cols in enumerate(halves):
+            nc.vector.tensor_copy(xq_w[:, cols], words[:].indirect(offs_sb[:, 16 * h : 16 * h + 16]))
+        a_words = dealt_words(ca_sb, "a_words", "a_words")
         ident = keep.tile([P, P], F32, name="ident")
         make_identity(nc, ident[:])
 
@@ -98,101 +110,133 @@ def tile_picked_ccmpclampbhopd_none_p_kernel(tc, x_words, x_scales, w1, gs, offs
         win_b = [keep.tile([P, WINDOW], F32, name="win_b%d" % t) for t in range(PACK)]
         plain_y = [keep.tile([P, S], F32, name="plain_y%d" % t) for t in range(PACK)]
         sig = [keep.tile([P, S], F32, name="sig%d" % t) for t in range(PACK)]
-        z_bf = keep.tile([P, PACK, S], BF16, name="z_bf")
+        z_bf = keep.tile([P, 2, PACK, S // 2], BF16, name="z_bf")
 
-        for t in range(PACK):
-            cols = slice(t * P, (t + 1) * P)
-            nc.tensor.matmul_mx(out=banks[t][:], lhsT=w_w[:, cols].bitcast(FP8X4), lhsT_scale=w_s[:, cols],
-                                rhs=xq_w[:].bitcast(FP8X4), rhs_scale=xq_s[:], start=True, stop=True)
-        for t in range(PACK):
-            nc.scalar.copy(win_a[t][:, :S], banks[t][:])
-            if t < 2:
-                nc.scalar.copy(plain_y[t][:], banks[t][:])
-            else:
-                nc.vector.tensor_copy(plain_y[t][:], win_a[t][:, :S])
+        def project(bank, t, cols):
+            rows = slice(t * P, (t + 1) * P)
+            nc.tensor.matmul_mx(out=bank[:, cols], lhsT=w_w[:, rows].bitcast(FP8X4), lhsT_scale=w_s[:, rows],
+                                rhs=xq_w[:, cols].bitcast(FP8X4), rhs_scale=xq_s[:, cols], start=True, stop=True)
+            nc.scalar.copy(win_a[t][:, cols], bank[:, cols])
+
+        project(banks[1], 1, halves[0])
+        project(banks[4], 1, halves[1])
+        project(banks[0], 0, whole)
+        nc.scalar.copy(plain_y[0][:], banks[0][:])
+        for t in (2, 3):
+            project(banks[t], t, whole)
+        for t in (1, 2, 3):
+            nc.vector.tensor_copy(plain_y[t][:], win_a[t][:, :S])
         for t in range(PACK):
             nc.vector.tensor_tensor(win_b[t][:, :S], win_a[t][:].indirect(n1_sb[:]), plain_y[t][:], ALU.subtract)
         for t in range(PACK):
             nc.scalar.activation(sig[t][:], win_b[t][:].indirect(n2_sb[:]), ACT.Sigmoid)
-        for t in range(PACK):
-            nc.vector.scalar_tensor_tensor(z_bf[:, t, :], plain_y[t][:], gs_sb[:, t : t + 1], sig[t][:], ALU.mult, ALU.mult)
+        for t in range(PACK - 1):
+            nc.vector.scalar_tensor_tensor(z_bf[:, :, t, :], plain_y[t][:].rearrange("p (h c) -> p h c", h=2), gs_sb[:, t : t + 1],
+                                           sig[t][:].rearrange("p (h c) -> p h c", h=2), ALU.mult, ALU.mult)
+        t = PACK - 1
+        for h, cols in enumerate(halves):
+            nc.vector.scalar_tensor_tensor(z_bf[:, h, t, :], plain_y[t][:, cols], gs_sb[:, t : t + 1], sig[t][:, cols], ALU.mult, ALU.mult)
 
-        z_il = [keep.tile([P, S // 2, PACK], BF16, name="z_il%d" % h, align_bytes=64) for h in range(2)]
+        z_il = [keep.tile([P, S // 2, PACK], BF16, name="z_il%d" % h, tag="z_il%d" % h, align_bytes=64) for h in range(2)]
         z_w = keep.tile([P, S], U32, name="z_w", align_bytes=64)
         z_s = keep.tile([P, S], U8, name="z_s", align_bytes=64)
-        halves = (slice(0, S // 2), slice(S // 2, S))
-        for engine_copy, half, cols in zip((nc.vector.tensor_copy, nc.scalar.copy), z_il, halves):
-            engine_copy(half[:].rearrange("p (c i) t -> p c t i", i=4), z_bf[:, :, cols].rearrange("p t (c i) -> p c t i", i=4))
+        for h, engine_copy in enumerate((nc.vector.tensor_copy, nc.scalar.copy)):
+            engine_copy(z_il[h][:].rearrange("p (c i) t -> p c t i", i=4), z_bf[:, h].rearrange("p t (c i) -> p c t i", i=4))
         for half, cols in zip(z_il, halves):
             nc.vector.quantize_mx(out=z_w[:, cols].bitcast(FP8X4), scales=z_s[:, cols], in_=half[:].rearrange("p c t -> p (c t)"))
 
+        b_words = dealt_words(cb_sb, "b_words", "z_il1")
+        dealt_w = (a_words, b_words)
+        dealt_s = (a_bytes, b_bytes)
+
         def product(bank, k, t, cols):
             rows = slice(t * P, (t + 1) * P)
-            nc.tensor.matmul_mx(out=bank[:, cols], lhsT=dealt_w[:, k, rows].bitcast(FP8X4), lhsT_scale=dealt_s[k][:, rows],
+            nc.tensor.matmul_mx(out=bank[:, cols], lhsT=dealt_w[k][:, rows].bitcast(FP8X4), lhsT_scale=dealt_s[k][:, rows],
                                 rhs=z_w[:, cols].bitcast(FP8X4), rhs_scale=z_s[:, cols], start=True, stop=True)
 
         out_rows = out.rearrange("(g t q) j -> t g q j", t=4, g=8)
-        whole = slice(0, S)
         plain_a = [keep.tile([P, S], F32, name="plain_a%d" % t) for t in range(PACK)]
         u = [keep.tile([P, S], F32, name="u%d" % t) for t in range(PACK)]
         d4 = [keep.tile([P, S], F32, name="d4_%d" % t) for t in range(PACK)]
         d5 = [keep.tile([P, S], F32, name="d5_%d" % t) for t in range(PACK)]
         res = [keep.tile([P, S], F32, name="res%d" % t) for t in range(PACK)]
         turned = [keep.tile([P, S], F32, name="turned%d" % t) for t in range(PACK - 1)]
-        ab_banks = ((4, 5), (0, 1), (2, 3), (4, 5))
+        over = [keep.tile([P, S], F32, name="over%d" % t) for t in range(2)]
+        lift = [keep.tile([P, S], F32, name="lift%d" % t) for t in range(2)]
 
-        def scores(t):
-            bank_a, bank_b = banks[ab_banks[t][0]], banks[ab_banks[t][1]]
-            if t == 0:
-                for bank, cols in zip((bank_a, banks[6]), halves):
-                    product(bank, 0, t, cols)
-                    nc.scalar.activation(win_a[t][:, cols], bank[:, cols], ACT.Copy, scale=-0.5 * 0.0625)
-                    nc.vector.tensor_scalar(plain_a[t][:, cols], win_a[t][:, cols], -2.0, None, ALU.mult)
-            else:
-                product(bank_a, 0, t, whole)
-                nc.scalar.activation(win_a[t][:, :S], bank_a[:], ACT.Copy, scale=-0.5 * 0.0625)
-                nc.scalar.activation(plain_a[t][:], bank_a[:], ACT.Copy, scale=0.0625)
-            product(bank_b, 1, t, whole)
-            nc.scalar.activation(win_b[t][:, :S], bank_b[:], ACT.Copy, scale=0.0625)
+        def score_a(t, bank, cols):
+            product(bank, 0, t, cols)
+            nc.scalar.activation(win_a[t][:, cols], bank[:, cols], ACT.Copy, scale=-0.5 * 0.0625)
+            nc.scalar.activation(plain_a[t][:, cols], bank[:, cols], ACT.Copy, scale=0.0625)
 
-        def first_gather(t):
+        def score_b(t, bank):
+            product(bank, 1, t, whole)
+            nc.scalar.activation(win_b[t][:, :S], bank[:], ACT.Copy, scale=0.0625)
+
+        def a_gather(t):
             nc.vector.tensor_tensor(u[t][:], win_a[t][:].indirect(n3_sb[:]), plain_a[t][:], ALU.add)
 
         def b_gathers(t):
             nc.vector.tensor_tensor(d4[t][:], win_b[t][:].indirect(n4_sb[:]), u[t][:], ALU.subtract)
             nc.vector.tensor_tensor(d5[t][:], win_b[t][:].indirect(n5_sb[:]), u[t][:], ALU.subtract)
 
-        def clamp(t):
+        def turn_and_add(bank, half, first, second):
+            for c in range(half.start, half.stop, P):
+                cols = slice(c, c + P)
+                nc.tensor.matmul(bank[:, cols], first[:, cols], ident[:], start=True, stop=False, is_transpose=True)
+                nc.tensor.matmul(bank[:, cols], second[:, cols], ident[:], start=False, stop=True, is_transpose=True)
+
+        def excess(t):
+            nc.scalar.activation(over[t][:], d4[t][:], ACT.Relu, scale=-1.0)
+
+        def combine_and_store(t):
+            for h, half in enumerate(halves):
+                turn_and_add(banks[h], half, u[t], d5[t])
+                nc.scalar.copy(turned[t][:, half], banks[h][:, half])
+                turn_and_add(banks[6 + h], half, d5[t], over[t])
+                nc.scalar.activation(lift[t][:, half], banks[6 + h][:, half], ACT.Relu, scale=-1.0)
+            for h, half in enumerate(halves):
+                turn_and_add(banks[2 + h], half, turned[t], lift[t])
+                nc.scalar.copy(res[t][:, half], banks[2 + h][:, half])
+            nc.scalar.dma_start(out_rows[t], res[t][:])
+
+        def clamp_and_store(t):
             nc.vector.scalar_tensor_tensor(d4[t][:], d4[t][:], 0.0, d5[t][:], ALU.min, ALU.max)
-
-        def add_and_store(t):
             for h, half in enumerate(halves):
-                blocks = [slice(c * P, (c + 1) * P) for c in (2 * h, 2 * h + 1)]
-                for cols in blocks:
-                    nc.tensor.matmul(banks[6 + h][:, cols], u[t][:, cols], ident[:], start=True, stop=False, is_transpose=True)
-                    nc.tensor.matmul(banks[6 + h][:, cols], d4[t][:, cols], ident[:], start=False, stop=True, is_transpose=True)
-                nc.scalar.copy(turned[t][:, half], banks[6 + h][:, half])
+                turn_and_add(banks[4 + h], half, u[t], d4[t])
+                nc.scalar.copy(turned[t][:, half], banks[4 + h][:, half])
             for h, half in enumerate(halves):
-                blocks = [slice(c * P, (c + 1) * P) for c in (2 * h, 2 * h + 1)]
-                for cols in blocks:
-                    nc.tensor.transpose(banks[h][:, cols], turned[t][:, cols], ident[:])
+                for c in range(half.start, half.stop, P):
+                    nc.tensor.transpose(banks[h][:, c : c + P], turned[t][:, c : c + P], ident[:])
                 nc.scalar.copy(res[t][:, half], banks[h][:, half])
-                nc.sync.dma_start(out_rows[t][:, :, half], res[t][:, half])
+            nc.scalar.dma_start(out_rows[t], res[t][:])
 
-        scores(0)
-        scores(1)
-        first_gather(0)
-        for t in range(PACK - 1):
-            b_gathers(t)
-            if t + 2 < PACK:
-                scores(t + 2)
-            first_gather(t + 1)
-            clamp(t)
-            add_and_store(t)
+        score_a(0, banks[4], halves[0])
+        score_a(0, banks[6], halves[1])
+        score_a(1, banks[0], whole)
+        score_b(0, banks[5])
+        a_gather(0)
+        a_gather(1)
+        b_gathers(0)
+        score_a(2, banks[1], whole)
+        score_b(1, banks[2])
+        excess(0)
+        score_b(2, banks[3])
+        score_a(3, banks[4], whole)
+        score_b(3, banks[5])
+        a_gather(2)
+        b_gathers(1)
+        b_gathers(2)
+        a_gather(3)
+        combine_and_store(0)
+        excess(1)
+        combine_and_store(1)
+        clamp_and_store(2)
         t = PACK - 1
         nc.vector.tensor_copy(d4[t][:], win_b[t][:].indirect(n4_sb[:]))
         nc.vector.tensor_copy(d5[t][:], win_b[t][:].indirect(n5_sb[:]))
-        nc.vector.tensor_tensor(d4[t][:], d4[t][:], u[t][:], ALU.min)
+        for cols in halves:
+            nc.vector.tensor_tensor(d4[t][:, cols], d4[t][:, cols], u[t][:, cols], ALU.min)
         for cols in halves:
             nc.vector.tensor_tensor(res[t][:, cols], d4[t][:, cols], d5[t][:, cols], ALU.max)
             nc.sync.dma_start(out_rows[t][:, :, cols], res[t][:, cols])

@@ -35,9 +35,6 @@ def tile_picked_ccmpclampbhopd_none_p_kernel(tc, x_words, x_scales, w1, gs, offs
 
         scales = keep.tile([P, T], U8, name="scales")
         nc.vector.memset(scales[:].bitcast(I32), 0)
-        warm = keep.tile([P, 8], F32, name="warm")
-        nc.gpsimd.memset(warm[:, 0:1], 0.0)
-        nc.scalar.activation(warm[:, 1:2], warm[:, 0:1], ACT.Sigmoid)
 
         offs_sb = load_list(offs, "offs_sb")
         ca_sb = load_list(ca, "ca_sb")
@@ -61,10 +58,8 @@ def tile_picked_ccmpclampbhopd_none_p_kernel(tc, x_words, x_scales, w1, gs, offs
         n4_sb = load_list(n4, "n4_sb")
         n5_sb = load_list(n5, "n5_sb")
 
-        def dealt_words(lst, name, tag):
-            dealt = keep.tile([P, S], U32, name=name, tag=tag, align_bytes=64)
-            nc.vector.tensor_copy(dealt[:].rearrange("p (t g q) -> p g t q", t=4, g=8), words[:].indirect(lst[:]))
-            return dealt
+        def deal_words(dealt, lst):
+            nc.vector.tensor_copy(dealt.rearrange("p (t g q) -> p g t q", t=4, g=16), words[:].indirect(lst[:]))
 
         def gathered_bytes(lst, name):
             picked = keep.tile([P, S], U8, name=name, align_bytes=64)
@@ -74,8 +69,8 @@ def tile_picked_ccmpclampbhopd_none_p_kernel(tc, x_words, x_scales, w1, gs, offs
         def dealt_bytes(picked, name):
             dealt = keep.tile([P, S], U8, name=name, align_bytes=64)
             nc.vector.tensor_copy(
-                dealt[:].bitcast(I32).rearrange("p (t g q) -> p t g q", t=4, g=8),
-                picked[:].bitcast(I32).rearrange("p (g t q) -> p t g q", t=4, g=8),
+                dealt[:].bitcast(I32).rearrange("p (t g q) -> p t g q", t=4, g=16),
+                picked[:].bitcast(I32).rearrange("p (g t q) -> p t g q", t=4, g=16),
             )
             return dealt
 
@@ -87,7 +82,7 @@ def tile_picked_ccmpclampbhopd_none_p_kernel(tc, x_words, x_scales, w1, gs, offs
         a_bytes = dealt_bytes(a_picked, "a_bytes")
         b_bytes = dealt_bytes(b_picked, "b_bytes")
 
-        w_bf = keep.tile([P, PACK, P, PACK], BF16, name="w_bf", align_bytes=64)
+        w_bf = keep.tile([P, PACK, P, PACK], BF16, name="w_bf", tag="w_bf", align_bytes=64)
         mw = cw // PACK
         for h in range(W_CHUNKS):
             nc.scalar.copy(
@@ -98,38 +93,41 @@ def tile_picked_ccmpclampbhopd_none_p_kernel(tc, x_words, x_scales, w1, gs, offs
         w_s = keep.tile([P, S], U8, name="w_s", align_bytes=64)
         nc.vector.quantize_mx(out=w_w[:].bitcast(FP8X4), scales=w_s[:], in_=w_bf[:].rearrange("p t m j -> p (t m j)"))
 
-        xq_w = keep.tile([P, S], U32, name="xq_w", align_bytes=64)
+        picked_words = keep.tile([P, 2 * S], U32, name="picked_words", tag="w_bf", align_bytes=64)
+        xq_w = picked_words[:, :S]
+        a_words = picked_words[:, S:]
         for h, cols in enumerate(halves):
             nc.vector.tensor_copy(xq_w[:, cols], words[:].indirect(offs_sb[:, 16 * h : 16 * h + 16]))
-        a_words = dealt_words(ca_sb, "a_words", "a_words")
+        deal_words(a_words, ca_sb)
         ident = keep.tile([P, P], F32, name="ident")
         make_identity(nc, ident[:])
 
         banks = [psum.tile([P, S], F32, name="bank%d" % b) for b in range(8)]
         win_a = [keep.tile([P, WINDOW], F32, name="win_a%d" % t) for t in range(PACK)]
         win_b = [keep.tile([P, WINDOW], F32, name="win_b%d" % t) for t in range(PACK)]
+        win_y = [keep.tile([P, WINDOW], F32, name="win_y%d" % t, tag="win_y%d" % t) for t in range(PACK)]
         plain_y = [keep.tile([P, S], F32, name="plain_y%d" % t) for t in range(PACK)]
         sig = [keep.tile([P, S], F32, name="sig%d" % t) for t in range(PACK)]
-        z_bf = keep.tile([P, 2, PACK, S // 2], BF16, name="z_bf")
 
         def project(bank, t, cols):
             rows = slice(t * P, (t + 1) * P)
             nc.tensor.matmul_mx(out=bank[:, cols], lhsT=w_w[:, rows].bitcast(FP8X4), lhsT_scale=w_s[:, rows],
                                 rhs=xq_w[:, cols].bitcast(FP8X4), rhs_scale=xq_s[:, cols], start=True, stop=True)
-            nc.scalar.copy(win_a[t][:, cols], bank[:, cols])
+            nc.scalar.copy(win_y[t][:, cols], bank[:, cols])
 
-        project(banks[1], 1, halves[0])
-        project(banks[4], 1, halves[1])
-        project(banks[0], 0, whole)
-        nc.scalar.copy(plain_y[0][:], banks[0][:])
+        project(banks[0], 0, halves[0])
+        project(banks[4], 0, halves[1])
+        nc.vector.tensor_copy(plain_y[0][:], win_y[0][:, :S])
+        project(banks[1], 1, whole)
+        nc.vector.tensor_copy(plain_y[1][:], win_y[1][:, :S])
         for t in (2, 3):
             project(banks[t], t, whole)
-        for t in (1, 2, 3):
-            nc.vector.tensor_copy(plain_y[t][:], win_a[t][:, :S])
+            nc.sync.dma_start(plain_y[t][:], win_y[t][:, :S])
         for t in range(PACK):
-            nc.vector.tensor_tensor(win_b[t][:, :S], win_a[t][:].indirect(n1_sb[:]), plain_y[t][:], ALU.subtract)
+            nc.vector.tensor_tensor(win_b[t][:, :S], win_y[t][:].indirect(n1_sb[:]), plain_y[t][:], ALU.subtract)
         for t in range(PACK):
             nc.scalar.activation(sig[t][:], win_b[t][:].indirect(n2_sb[:]), ACT.Sigmoid)
+        z_bf = keep.tile([P, 2, PACK, S // 2], BF16, name="z_bf", tag="win_y3")
         for t in range(PACK - 1):
             nc.vector.scalar_tensor_tensor(z_bf[:, :, t, :], plain_y[t][:].rearrange("p (h c) -> p h c", h=2), gs_sb[:, t : t + 1],
                                            sig[t][:].rearrange("p (h c) -> p h c", h=2), ALU.mult, ALU.mult)
@@ -145,7 +143,8 @@ def tile_picked_ccmpclampbhopd_none_p_kernel(tc, x_words, x_scales, w1, gs, offs
         for half, cols in zip(z_il, halves):
             nc.vector.quantize_mx(out=z_w[:, cols].bitcast(FP8X4), scales=z_s[:, cols], in_=half[:].rearrange("p c t -> p (c t)"))
 
-        b_words = dealt_words(cb_sb, "b_words", "z_il1")
+        b_words = keep.tile([P, S], U32, name="b_words", tag="z_il1", align_bytes=64)
+        deal_words(b_words[:], cb_sb)
         dealt_w = (a_words, b_words)
         dealt_s = (a_bytes, b_bytes)
 
@@ -154,7 +153,7 @@ def tile_picked_ccmpclampbhopd_none_p_kernel(tc, x_words, x_scales, w1, gs, offs
             nc.tensor.matmul_mx(out=bank[:, cols], lhsT=dealt_w[k][:, rows].bitcast(FP8X4), lhsT_scale=dealt_s[k][:, rows],
                                 rhs=z_w[:, cols].bitcast(FP8X4), rhs_scale=z_s[:, cols], start=True, stop=True)
 
-        out_rows = out.rearrange("(g t q) j -> t g q j", t=4, g=8)
+        out_rows = out.rearrange("(g t q) j -> t g q j", t=4, g=16)
         plain_a = [keep.tile([P, S], F32, name="plain_a%d" % t) for t in range(PACK)]
         u = [keep.tile([P, S], F32, name="u%d" % t) for t in range(PACK)]
         d4 = [keep.tile([P, S], F32, name="d4_%d" % t) for t in range(PACK)]

from contextlib import ExitStack

import concourse.mybir as mybir
from concourse.masks import make_identity

F32 = mybir.dt.float32
BF16 = mybir.dt.bfloat16
I32 = mybir.dt.int32
U32 = mybir.dt.uint32
U16 = mybir.dt.uint16
U8 = mybir.dt.uint8
FP8X4 = mybir.dt.float8_e4m3fn_x4
ALU = mybir.AluOpType
ACT = mybir.ActivationFunctionType

P = 128
T = 2048
S = 512
PACK = 4
WINDOW = 1024
W_CHUNKS = 2
FLOPS = 3 * 2 * 512 * 512 * 512


def tile_picked_ccmpclampbhopd_none_p_kernel(tc, x_words, x_scales, w1, gs, offs, n1, n2, ca, cb, n3, n4, n5, out):
    nc = tc.nc
    with ExitStack() as ctx:
        keep = ctx.enter_context(tc.tile_pool(name="keep", bufs=1))
        psum = ctx.enter_context(tc.psum_pool(name="psum", bufs=1))

        def load_list(src, name):
            tile = keep.tile([P, S // 16], U16, name=name)
            nc.sync.dma_start(tile[:], src)
            return tile

        scales = keep.tile([P, T], U8, name="scales")
        nc.vector.memset(scales[:].bitcast(I32), 0)

        offs_sb = load_list(offs, "offs_sb")
        ca_sb = load_list(ca, "ca_sb")
        cb_sb = load_list(cb, "cb_sb")
        for q in range(4):
            nc.sync.dma_start(scales[32 * q : 32 * q + 4, :].bitcast(I32), x_scales[0, 4 * q : 4 * q + 4, :].bitcast(I32))
        cw = S // W_CHUNKS
        w_rows = w1.rearrange("(p j) c -> p j c", j=PACK)
        w_raw = []
        for h in range(W_CHUNKS):
            tile = keep.tile([P, PACK, cw], F32, name="w_raw%d" % h)
            nc.sync.dma_start(tile[:], w_rows[:, :, h * cw : (h + 1) * cw])
            w_raw.append(tile)
        words = keep.tile([P, T], U32, name="words", align_bytes=64)
        nc.sync.dma_start(words[:].bitcast(I32), x_words[0].rearrange("p n t -> p (n t)").bitcast(I32))
        n1_sb = load_list(n1, "n1_sb")
        n2_sb = load_list(n2, "n2_sb")
        gs_sb = keep.tile([P, PACK], F32, name="gs_sb")
        nc.sync.dma_start(gs_sb[:], gs.rearrange("(p t) o -> p (t o)", t=PACK))
        n3_sb = load_list(n3, "n3_sb")
        n4_sb = load_list(n4, "n4_sb")
        n5_sb = load_list(n5, "n5_sb")

        def deal_words(dealt, lst):
            nc.vector.tensor_copy(dealt.rearrange("p (t g q) -> p g t q", t=4, g=16), words[:].indirect(lst[:]))

        def gathered_bytes(lst, name):
            picked = keep.tile([P, S], U8, name=name, align_bytes=64)
            nc.vector.tensor_copy(picked[:], scales[:].indirect(lst[:]))
            return picked

        def dealt_bytes(picked, name):
            dealt = keep.tile([P, S], U8, name=name, align_bytes=64)
            nc.vector.tensor_copy(
                dealt[:].bitcast(I32).rearrange("p (t g q) -> p t g q", t=4, g=16),
                picked[:].bitcast(I32).rearrange("p (g t q) -> p t g q", t=4, g=16),
            )
            return dealt

        halves = (slice(0, S // 2), slice(S // 2, S))
        whole = slice(0, S)
        xq_s = gathered_bytes(offs_sb, "xq_s")
        a_picked = gathered_bytes(ca_sb, "a_picked")
        b_picked = gathered_bytes(cb_sb, "b_picked")
        a_bytes = dealt_bytes(a_picked, "a_bytes")
        b_bytes = dealt_bytes(b_picked, "b_bytes")

        w_bf = keep.tile([P, PACK, P, PACK], BF16, name="w_bf", tag="w_bf", align_bytes=64)
        mw = cw // PACK
        for h in range(W_CHUNKS):
            nc.scalar.copy(
                w_bf[:, :, h * mw : (h + 1) * mw, :].rearrange("p t m j -> p m t j"),
                w_raw[h][:].rearrange("p j (m t) -> p m t j", t=PACK),
            )
        w_w = keep.tile([P, S], U32, name="w_w", align_bytes=64)
        w_s = keep.tile([P, S], U8, name="w_s", align_bytes=64)
        nc.vector.quantize_mx(out=w_w[:].bitcast(FP8X4), scales=w_s[:], in_=w_bf[:].rearrange("p t m j -> p (t m j)"))

        picked_words = keep.tile([P, 2 * S], U32, name="picked_words", tag="w_bf", align_bytes=64)
        xq_w = picked_words[:, :S]
        a_words = picked_words[:, S:]
        for h, cols in enumerate(halves):
            nc.vector.tensor_copy(xq_w[:, cols], words[:].indirect(offs_sb[:, 16 * h : 16 * h + 16]))
        deal_words(a_words, ca_sb)
        ident = keep.tile([P, P], F32, name="ident")
        make_identity(nc, ident[:])

        banks = [psum.tile([P, S], F32, name="bank%d" % b) for b in range(8)]
        win_a = [keep.tile([P, WINDOW], F32, name="win_a%d" % t) for t in range(PACK)]
        win_b = [keep.tile([P, WINDOW], F32, name="win_b%d" % t) for t in range(PACK)]
        win_y = [keep.tile([P, WINDOW], F32, name="win_y%d" % t, tag="win_y%d" % t) for t in range(PACK)]
        plain_y = [keep.tile([P, S], F32, name="plain_y%d" % t) for t in range(PACK)]
        sig = [keep.tile([P, S], F32, name="sig%d" % t) for t in range(PACK)]

        def project(bank, t, cols):
            rows = slice(t * P, (t + 1) * P)
            nc.tensor.matmul_mx(out=bank[:, cols], lhsT=w_w[:, rows].bitcast(FP8X4), lhsT_scale=w_s[:, rows],
                                rhs=xq_w[:, cols].bitcast(FP8X4), rhs_scale=xq_s[:, cols], start=True, stop=True)
            nc.scalar.copy(win_y[t][:, cols], bank[:, cols])

        project(banks[0], 0, halves[0])
        project(banks[4], 0, halves[1])
        nc.vector.tensor_copy(plain_y[0][:], win_y[0][:, :S])
        project(banks[1], 1, whole)
        nc.vector.tensor_copy(plain_y[1][:], win_y[1][:, :S])
        for t in (2, 3):
            project(banks[t], t, whole)
            nc.sync.dma_start(plain_y[t][:], win_y[t][:, :S])
        for t in range(PACK):
            nc.vector.tensor_tensor(win_b[t][:, :S], win_y[t][:].indirect(n1_sb[:]), plain_y[t][:], ALU.subtract)
        for t in range(PACK):
            nc.scalar.activation(sig[t][:], win_b[t][:].indirect(n2_sb[:]), ACT.Sigmoid)
        z_bf = keep.tile([P, 2, PACK, S // 2], BF16, name="z_bf", tag="win_y3")
        for t in range(PACK - 1):
            nc.vector.scalar_tensor_tensor(z_bf[:, :, t, :], plain_y[t][:].rearrange("p (h c) -> p h c", h=2), gs_sb[:, t : t + 1],
                                           sig[t][:].rearrange("p (h c) -> p h c", h=2), ALU.mult, ALU.mult)
        t = PACK - 1
        for h, cols in enumerate(halves):
            nc.vector.scalar_tensor_tensor(z_bf[:, h, t, :], plain_y[t][:, cols], gs_sb[:, t : t + 1], sig[t][:, cols], ALU.mult, ALU.mult)

        z_il = [keep.tile([P, S // 2, PACK], BF16, name="z_il%d" % h, tag="z_il%d" % h, align_bytes=64) for h in range(2)]
        z_w = keep.tile([P, S], U32, name="z_w", align_bytes=64)
        z_s = keep.tile([P, S], U8, name="z_s", align_bytes=64)
        for h, engine_copy in enumerate((nc.vector.tensor_copy, nc.scalar.copy)):
            engine_copy(z_il[h][:].rearrange("p (c i) t -> p c t i", i=4), z_bf[:, h].rearrange("p t (c i) -> p c t i", i=4))
        for half, cols in zip(z_il, halves):
            nc.vector.quantize_mx(out=z_w[:, cols].bitcast(FP8X4), scales=z_s[:, cols], in_=half[:].rearrange("p c t -> p (c t)"))

        b_words = keep.tile([P, S], U32, name="b_words", tag="z_il1", align_bytes=64)
        deal_words(b_words[:], cb_sb)
        dealt_w = (a_words, b_words)
        dealt_s = (a_bytes, b_bytes)

        def product(bank, k, t, cols):
            rows = slice(t * P, (t + 1) * P)
            nc.tensor.matmul_mx(out=bank[:, cols], lhsT=dealt_w[k][:, rows].bitcast(FP8X4), lhsT_scale=dealt_s[k][:, rows],
                                rhs=z_w[:, cols].bitcast(FP8X4), rhs_scale=z_s[:, cols], start=True, stop=True)

        out_rows = out.rearrange("(g t q) j -> t g q j", t=4, g=16)
        plain_a = [keep.tile([P, S], F32, name="plain_a%d" % t) for t in range(PACK)]
        u = [keep.tile([P, S], F32, name="u%d" % t) for t in range(PACK)]
        d4 = [keep.tile([P, S], F32, name="d4_%d" % t) for t in range(PACK)]
        d5 = [keep.tile([P, S], F32, name="d5_%d" % t) for t in range(PACK)]
        res = [keep.tile([P, S], F32, name="res%d" % t) for t in range(PACK)]
        turned = [keep.tile([P, S], F32, name="turned%d" % t) for t in range(PACK - 1)]
        over = [keep.tile([P, S], F32, name="over%d" % t) for t in range(2)]
        lift = [keep.tile([P, S], F32, name="lift%d" % t) for t in range(2)]

        def score_a(t, bank, cols):
            product(bank, 0, t, cols)
            nc.scalar.activation(win_a[t][:, cols], bank[:, cols], ACT.Copy, scale=-0.5 * 0.0625)
            nc.scalar.activation(plain_a[t][:, cols], bank[:, cols], ACT.Copy, scale=0.0625)

        def score_b(t, bank):
            product(bank, 1, t, whole)
            nc.scalar.activation(win_b[t][:, :S], bank[:], ACT.Copy, scale=0.0625)

        def a_gather(t):
            nc.vector.tensor_tensor(u[t][:], win_a[t][:].indirect(n3_sb[:]), plain_a[t][:], ALU.add)

        def b_gathers(t):
            nc.vector.tensor_tensor(d4[t][:], win_b[t][:].indirect(n4_sb[:]), u[t][:], ALU.subtract)
            nc.vector.tensor_tensor(d5[t][:], win_b[t][:].indirect(n5_sb[:]), u[t][:], ALU.subtract)

        def turn_and_add(bank, half, first, second):
            for c in range(half.start, half.stop, P):
                cols = slice(c, c + P)
                nc.tensor.matmul(bank[:, cols], first[:, cols], ident[:], start=True, stop=False, is_transpose=True)
                nc.tensor.matmul(bank[:, cols], second[:, cols], ident[:], start=False, stop=True, is_transpose=True)

        def excess(t):
            nc.scalar.activation(over[t][:], d4[t][:], ACT.Relu, scale=-1.0)

        def combine_and_store(t):
            for h, half in enumerate(halves):
                turn_and_add(banks[h], half, u[t], d5[t])
                nc.scalar.copy(turned[t][:, half], banks[h][:, half])
                turn_and_add(banks[6 + h], half, d5[t], over[t])
                nc.scalar.activation(lift[t][:, half], banks[6 + h][:, half], ACT.Relu, scale=-1.0)
            for h, half in enumerate(halves):
                turn_and_add(banks[2 + h], half, turned[t], lift[t])
                nc.scalar.copy(res[t][:, half], banks[2 + h][:, half])
            nc.scalar.dma_start(out_rows[t], res[t][:])

        def clamp_and_store(t):
            nc.vector.scalar_tensor_tensor(d4[t][:], d4[t][:], 0.0, d5[t][:], ALU.min, ALU.max)
            for h, half in enumerate(halves):
                turn_and_add(banks[4 + h], half, u[t], d4[t])
                nc.scalar.copy(turned[t][:, half], banks[4 + h][:, half])
            for h, half in enumerate(halves):
                for c in range(half.start, half.stop, P):
                    nc.tensor.transpose(banks[h][:, c : c + P], turned[t][:, c : c + P], ident[:])
                nc.scalar.copy(res[t][:, half], banks[h][:, half])
            nc.scalar.dma_start(out_rows[t], res[t][:])

        score_a(0, banks[4], halves[0])
        score_a(0, banks[6], halves[1])
        score_a(1, banks[0], whole)
        score_b(0, banks[5])
        a_gather(0)
        a_gather(1)
        b_gathers(0)
        score_a(2, banks[1], whole)
        score_b(1, banks[2])
        excess(0)
        score_b(2, banks[3])
        score_a(3, banks[4], whole)
        score_b(3, banks[5])
        a_gather(2)
        b_gathers(1)
        b_gathers(2)
        a_gather(3)
        combine_and_store(0)
        excess(1)
        combine_and_store(1)
        clamp_and_store(2)
        t = PACK - 1
        nc.vector.tensor_copy(d4[t][:], win_b[t][:].indirect(n4_sb[:]))
        nc.vector.tensor_copy(d5[t][:], win_b[t][:].indirect(n5_sb[:]))
        for cols in halves:
            nc.vector.tensor_tensor(d4[t][:, cols], d4[t][:, cols], u[t][:, cols], ALU.min)
        for cols in halves:
            nc.vector.tensor_tensor(res[t][:, cols], d4[t][:, cols], d5[t][:, cols], ALU.max)
            nc.sync.dma_start(out_rows[t][:, :, cols], res[t][:, cols])
